import numpy as np
import ml_dtypes


def mxq(x, axis, fmt="e4m3"):
    dtype, down = {"e4m3": (ml_dtypes.float8_e4m3fn, 7), "e5m2": (ml_dtypes.float8_e5m2, 14)}[fmt]
    v = np.moveaxis(np.asarray(x, np.float32).astype(ml_dtypes.bfloat16).astype(np.float64), axis, -1)
    blocks = v.reshape(v.shape[:-1] + (-1, 32))
    amax = np.abs(blocks).max(-1, keepdims=True)
    byte = np.maximum(np.where(amax > 0, np.frexp(amax)[1] - 1 + 127, 0) - down, 1)
    scale = np.exp2(byte - 127.0)
    codes = (blocks / scale).astype(np.float32).astype(dtype).astype(np.float64)
    return np.moveaxis((codes * scale).reshape(v.shape), -1, axis)


WIDE = False


def mx_kscale(k):
    if not WIDE:
        return np.ones(k)
    levels = np.array([10, -10, 5, -5, 0])
    if k % 512:
        return np.exp2(np.random.permutation(np.resize(levels, k // 32))).repeat(32)
    a = np.empty((k // 512, 16))
    for p in range(k // 512):
        a[p, :8] = np.random.permutation(np.resize(levels, 8))
        for g in range(8):
            far = levels[np.abs(levels - a[p, g]) >= 10]
            a[p, g + 8] = far[np.random.randint(len(far))]
    return np.exp2(a.ravel()).repeat(32)


BF16 = ml_dtypes.bfloat16


def bf(x):
    return np.asarray(x, np.float32).astype(BF16)


def f64(x):
    return np.asarray(x).astype(np.float64)


E2M1 = np.array([0.0, 0.5, 1.0, 1.5, 2.0, 3.0, 4.0, 6.0, -0.0, -0.5, -1.0, -1.5, -2.0, -3.0, -4.0, -6.0])


def pack_weight(w, fmt):
    k, n = w.shape
    w = f64(bf(w)).reshape(k // 32, 32, n)
    amax = np.abs(w).max(1)
    if fmt == "e4m3":
        byte = np.frexp(amax)[1] - 1 + 127 - 7
    else:
        mant, ex = np.frexp(amax / 6.0)
        byte = np.where(mant > 0.5, ex, ex - 1) + 127
    byte = np.clip(np.where(amax > 0, byte, 1), 1, 254)
    scaled = (w * np.exp2(127.0 - byte)[:, None, :]).reshape(k, n).astype(np.float32)
    by_word = np.ascontiguousarray(scaled.reshape(k // 512, 128, 4, n).transpose(0, 1, 3, 2))
    if fmt == "e4m3":
        words = by_word.astype(ml_dtypes.float8_e4m3fn).view(np.uint8)
    else:
        c = by_word.astype(ml_dtypes.float4_e2m1fn).view(np.uint8) & 0xF
        words = c[..., 0::2] | (c[..., 1::2] << 4)
    return np.ascontiguousarray(words), np.ascontiguousarray(byte.astype(np.uint8).reshape(k // 512, 16, n))


def unpack_weight(words, scales, fmt):
    g, p, n, _ = words.shape
    if fmt == "e4m3":
        vals = np.ascontiguousarray(words).view(ml_dtypes.float8_e4m3fn).astype(np.float64)
    else:
        nib = np.empty((g, p, n, 4), np.uint8)
        nib[..., 0::2] = words & 0xF
        nib[..., 1::2] = words >> 4
        vals = E2M1[nib]
    vals = vals * np.repeat(np.exp2(scales.astype(np.float64) - 127.0), 8, axis=1)[..., None]
    return vals.transpose(0, 1, 3, 2).reshape(g * 512, n)
def pack4(w):
    words, scales = pack_weight(w, "e2m1")
    return words.reshape(words.shape[0], 128, -1), scales


def unpack4(words, scales):
    return unpack_weight(words.reshape(words.shape[0], 128, -1, 2), scales, "e2m1")


N, D, F1, F2, F = 1024, 1024, 512, 1024, 2048


def draw0():
    s, t = mx_kscale(D), mx_kscale(F)
    x = bf(np.random.standard_normal((N, D)) * s)
    w_enc_words, w_enc_scales = pack4(np.random.standard_normal((D, F)) / np.sqrt(D) / s[:, None] * t)
    b_enc = bf(np.random.standard_normal(F) * 0.3 * t)
    w_dec_words, w_dec_scales = pack4(np.random.standard_normal((F, D)) / np.sqrt(F - F2) / t[:, None])
    return {
        "x": x,
        "w_enc_words": w_enc_words,
        "w_enc_scales": w_enc_scales,
        "b_enc": b_enc,
        "w_dec_words": w_dec_words,
        "w_dec_scales": w_dec_scales,
        "b_dec": bf(np.random.standard_normal(D) * 0.3),
        "y": bf(np.random.standard_normal((N, D))),
    }


def encode(x, w_enc_words, w_enc_scales, b_enc):
    return np.maximum((mxq(f64(x), 1, "e4m3") @ unpack4(w_enc_words, w_enc_scales)) + f64(b_enc), 0.0)


def decode_block(hq, wq, start, stop):
    return hq[:, start:stop] @ wq[start:stop, :]


def core(x, w_enc_words, w_enc_scales, b_enc, w_dec_words, w_dec_scales, b_dec, y):
    h = encode(x, w_enc_words, w_enc_scales, b_enc)
    hq = mxq(h, 1, "e4m3")
    wq = unpack4(w_dec_words, w_dec_scales)
    c1 = decode_block(hq, wq, 0, F1)
    c2 = decode_block(hq, wq, F1, F2)
    c3 = decode_block(hq, wq, F2, F)
    t = f64(y) - f64(b_dec)
    r1 = t - c1
    r2 = r1 - c2
    r3 = r2 - c3
    return np.stack([r1, r2, r3], axis=0)


def e4m3fn_bytes(y):
    return np.clip(np.asarray(y, np.float64), -448.0, 448.0).astype(np.float32).astype(ml_dtypes.float8_e4m3fn).view(np.uint8)


def e4m3fn_values(b):
    return np.asarray(b, np.uint8).view(ml_dtypes.float8_e4m3fn).astype(np.float64)


def setup_inputs():
    d = draw0()
    x0 = np.asarray(d['x']).astype(np.float64)
    s = (np.max(np.abs(x0), axis=(0,), keepdims=True) / 448.0).astype(np.float32)
    out = {}
    for k, v in d.items():
        if k == 'x':
            out['x_bytes'] = e4m3fn_bytes(x0 / s.astype(np.float64))
            out['x_scale'] = s
        else:
            out[k] = v
    return out


def reference(x_bytes, x_scale, w_enc_words, w_enc_scales, b_enc, w_dec_words, w_dec_scales, b_dec, y):
    return core(e4m3fn_values(x_bytes) * x_scale.astype(np.float64), w_enc_words, w_enc_scales, b_enc, w_dec_words, w_dec_scales, b_dec, y)

@@ -1,0 +1,240 @@
+from contextlib import ExitStack
+
+import concourse.mybir as mybir
+from concourse.masks import make_identity
+
+F32 = mybir.dt.float32
+BF16 = mybir.dt.bfloat16
+U8 = mybir.dt.uint8
+U16 = mybir.dt.uint16
+U32 = mybir.dt.uint32
+I32 = mybir.dt.int32
+FP8 = mybir.dt.float8_e4m3fn
+FP8X4 = mybir.dt.float8_e4m3fn_x4
+FP4X4 = mybir.dt.float4_e2m1fn_x4
+ALU = mybir.AluOpType
+ACT = mybir.ActivationFunctionType
+
+N, D, F = 1024, 1024, 2048
+FLOPS = 2 * N * D * F * 2
+P = 128
+CH = 512
+NCH = N // CH
+NJ = CH // P
+GE = D // 512
+GF = F // 512
+OFFLOAD = {(1, 2, 1, 0), (1, 2, 2, 0)}
+
+
+def tile_matryoshkatranscoderresiduals_w4_kernel(
+    tc, x_bytes, x_scale, w_enc_words, w_enc_scales, b_enc, w_dec_words, w_dec_scales, b_dec, y, out
+):
+    nc = tc.nc
+    with ExitStack() as ctx:
+        keep = ctx.enter_context(tc.tile_pool(name="keep", bufs=1))
+        work = ctx.enter_context(tc.tile_pool(name="work", bufs=3))
+        hpool = ctx.enter_context(tc.tile_pool(name="hpool", bufs=5))
+        rpool = ctx.enter_context(tc.tile_pool(name="rpool", bufs=5))
+        pe_pool = ctx.enter_context(tc.psum_pool(name="pe_pool", bufs=4))
+        pd_pool = ctx.enter_context(tc.psum_pool(name="pd_pool", bufs=4))
+
+        warm = keep.tile([P, 1], F32)
+        ident = keep.tile([P, P], F32)
+        xscale = keep.tile([P, D], F32)
+        benc = keep.tile([P, GF, 4], BF16)
+        bdec = keep.tile([P, D], BF16)
+        xb = [keep.tile([P, NJ, D], U8, name="xb%d" % c) for c in range(NCH)]
+        yt = [keep.tile([P, NJ, D], BF16, name="yt%d" % c) for c in range(NCH)]
+        wraw = [keep.tile([P, GE, 1024], U8, name="wraw%d" % f) for f in range(GF)]
+        wperm = [keep.tile([P, GE, 1024], U8, name="wperm%d" % f, align_bytes=64) for f in range(GF)]
+        wsraw = keep.tile([P, GE, F], U8)
+        wsperm = [keep.tile([P, GE, 512], U8, name="wsperm%d" % f, align_bytes=64) for f in range(GF)]
+        wd = keep.tile([P, GF, 2 * D], U8, align_bytes=64)
+        wds = keep.tile([P, GF, D], U8, align_bytes=64)
+        xcod = [keep.tile([P, GE, CH], U32, name="xcod%d" % c, align_bytes=64) for c in range(NCH)]
+        xcs = [keep.tile([P, GE, CH], U8, name="xcs%d" % c, align_bytes=64) for c in range(NCH)]
+
+        nc.vector.memset(wsraw[:].rearrange("p g n -> p (g n)").bitcast(I32), 0)
+        nc.vector.memset(wds[:].rearrange("p g n -> p (g n)").bitcast(I32), 0)
+        nc.vector.memset(warm[:], 0.0)
+        nc.scalar.dma_start(out=xscale[:], in_=x_scale.rearrange("o k -> (o k)").partition_broadcast(P))
+        nc.scalar.activation(out=warm[:], in_=warm[:], func=ACT.Relu)
+        make_identity(nc, ident[:])
+
+        xv = [x_bytes[c * CH : (c + 1) * CH, :].rearrange("(p j) k -> p j k", j=NJ) for c in range(NCH)]
+        yv = [y[c * CH : (c + 1) * CH, :].rearrange("(p j) k -> p j k", j=NJ) for c in range(NCH)]
+        ov = [[out[k, c * CH : (c + 1) * CH, :].rearrange("(p j) k -> p j k", j=NJ) for c in range(NCH)] for k in range(3)]
+
+        def load_w(f):
+            nc.sync.dma_start(
+                out=wraw[f][:].bitcast(I32),
+                in_=w_enc_words.bitcast(I32)[:, :, f * 256 : (f + 1) * 256].rearrange("g p n -> p g n"),
+            )
+
+        def load_scales(tile, src):
+            for q in range(4):
+                nc.sync.dma_start(
+                    out=tile[32 * q : 32 * q + 4].bitcast(I32),
+                    in_=src.bitcast(I32)[:, 4 * q : 4 * q + 4, :].rearrange("g q n -> q g n"),
+                )
+
+        nc.scalar.dma_start(out=benc[:], in_=b_enc.rearrange("(g p t) -> p g t", p=P, t=4))
+        nc.scalar.dma_start(out=bdec[:], in_=b_dec.partition_broadcast(P))
+        load_w(0)
+        nc.sync.dma_start(out=xb[0][:, 0:2, :], in_=xv[0][:, 0:2, :])
+        nc.sync.dma_start(out=xb[0][:, 2:4, :], in_=xv[0][:, 2:4, :])
+        load_scales(wsraw, w_enc_scales)
+        load_w(1)
+        nc.sync.dma_start(out=xb[1][:], in_=xv[1])
+        nc.sync.dma_start(out=yt[0][:], in_=yv[0])
+        load_w(2)
+        load_w(3)
+        nc.sync.dma_start(out=wd[:, 0:2, :].bitcast(I32), in_=w_dec_words[0:2].bitcast(I32).rearrange("g p n -> p g n"))
+        load_scales(wds, w_dec_scales)
+        nc.sync.dma_start(out=wd[:, 2:4, :].bitcast(I32), in_=w_dec_words[2:4].bitcast(I32).rearrange("g p n -> p g n"))
+        nc.sync.dma_start(out=yt[1][:], in_=yv[1])
+
+        def permute_words(f):
+            for g in range(GE):
+                nc.vector.tensor_copy(
+                    out=wperm[f][:, g, :].bitcast(U16).rearrange("p (t m) -> p t m", t=4),
+                    in_=wraw[f][:, g, :].bitcast(U16).rearrange("p (m t) -> p t m", t=4),
+                )
+        def permute_scales(f):
+            (nc.vector if f < 1 else nc.gpsimd).tensor_copy(
+                out=wsperm[f][:].rearrange("p g (t m) -> p g t m", t=4),
+                in_=wsraw[:, :, f * 512 : (f + 1) * 512].rearrange("p g (m t) -> p g t m", t=4),
+            )
+
+        def x_scale_rows(c, j):
+            xs = work.tile([P, D], BF16, name="xs")
+            nc.vector.tensor_tensor(out=xs[:], in0=xb[c][:, j, :].bitcast(FP8), in1=xscale[:], op=ALU.mult)
+            return xs
+
+        def x_turn(c, j, xs):
+            bank = pe_pool.tile([P, 4, P], F32, name="pe")
+            words = xs[:].bitcast(F32)
+            for g in range(GE):
+                for u in range(2):
+                    nc.tensor.transpose(bank[:, 2 * g + u, :], words[:, 256 * g + u : 256 * (g + 1) : 2], ident[:])
+            xin = work.tile([P, GE, P, 4], BF16, name="xin", align_bytes=64)
+            nc.scalar.copy(
+                out=xin[:].rearrange("p g n t -> p (g n t)").bitcast(F32).rearrange("p (g n u) -> p g n u", g=GE, u=2),
+                in_=bank[:].rearrange("p (g u) n -> p g n u", u=2),
+            )
+            return xin
+
+        def x_quant(c, j, xin):
+            for g in range(GE):
+                cols = slice(j * P, (j + 1) * P)
+                nc.vector.quantize_mx(
+                    out=xcod[c][:, g, cols].bitcast(FP8X4),
+                    scales=xcs[c][:, g, cols],
+                    in_=xin[:, g, :, :].rearrange("p n t -> p (n t)"),
+                )
+
+        hcod, hsc = {}, {}
+        hbuf = {}
+
+        def enc(c, f, t):
+            bank = pe_pool.tile([P, CH], F32, name="pe")
+            for g in range(GE):
+                nc.tensor.matmul_mx(
+                    out=bank[:],
+                    lhsT=wperm[f][:, g, 256 * t : 256 * (t + 1)].bitcast(FP4X4),
+                    lhsT_scale=wsperm[f][:, g, 128 * t : 128 * (t + 1)],
+                    rhs=xcod[c][:, g, :].bitcast(FP8X4),
+                    rhs_scale=xcs[c][:, g, :],
+                    start=(g == 0),
+                    stop=(g == GE - 1),
+                )
+            if t == 0:
+                hbuf[c, f] = work.tile([P, 2, CH, 2], BF16, name="hb")
+            nc.scalar.activation(
+                out=hbuf[c, f][:, t // 2, :, t % 2], in_=bank[:], func=ACT.Relu, bias=benc[:, f, t : t + 1]
+            )
+
+        hins = {}
+
+        def h_turn(c, f):
+            hin = work.tile([P, CH, 4], BF16, name="hin", align_bytes=64)
+            nc.scalar.copy(
+                out=hin[:].rearrange("p n t -> p (n t)").bitcast(F32).rearrange("p (n u) -> p n u", u=2),
+                in_=hbuf[c, f][:].rearrange("p u n e -> p (u n e)").bitcast(F32).rearrange("p (u n) -> p n u", u=2),
+            )
+            hins[c, f] = hin
+
+        def h_quant(c, f):
+            hcod[c, f] = hpool.tile([P, CH], U32, name="hcod", align_bytes=64)
+            hsc[c, f] = hpool.tile([P, CH], U8, name="hsc", align_bytes=64)
+            nc.vector.quantize_mx(
+                out=hcod[c, f][:].bitcast(FP8X4), scales=hsc[c, f][:], in_=hins[c, f][:].rearrange("p n t -> p (n t)")
+            )
+
+        res = {}
+
+        def target(c, j):
+            t = rpool.tile([P, D], F32, name="tgt")
+            nc.gpsimd.tensor_tensor(out=t[:], in0=yt[c][:, j, :], in1=bdec[:], op=ALU.subtract)
+            res[c, j] = t
+
+        def dec(c, k, j, d):
+            groups = ([0], [1], [2, 3])[k]
+            bank = pd_pool.tile([P, 512], F32, name="pd")
+            for i, f in enumerate(groups):
+                nc.tensor.matmul_mx(
+                    out=bank[:],
+                    lhsT=hcod[c, f][:, j * P : (j + 1) * P].bitcast(FP8X4),
+                    lhsT_scale=hsc[c, f][:, j * P : (j + 1) * P],
+                    rhs=wd[:, f, 1024 * d : 1024 * (d + 1)].bitcast(FP4X4),
+                    rhs_scale=wds[:, f, 512 * d : 512 * (d + 1)],
+                    start=(i == 0),
+                    stop=(i == len(groups) - 1),
+                )
+            if d == 0:
+                res[c, j, k] = rpool.tile([P, D], F32, name="r%d" % k)
+            prev = res[c, j] if k == 0 else res[c, j, k - 1]
+            cols = slice(512 * d, 512 * (d + 1))
+            if (c, k, j, d) in OFFLOAD:
+                part = work.tile([P, 512], F32, name="part")
+                nc.scalar.copy(out=part[:], in_=bank[:])
+                nc.gpsimd.tensor_tensor(out=res[c, j, k][:, cols], in0=prev[:, cols], in1=part[:], op=ALU.subtract)
+            else:
+                nc.vector.tensor_tensor(out=res[c, j, k][:, cols], in0=prev[:, cols], in1=bank[:], op=ALU.subtract)
+            if d == 1:
+                nc.sync.dma_start(out=ov[k][c][:, j, :], in_=res[c, j, k][:])
+
+        permute_words(0)
+        pend = [x_scale_rows(0, j) for j in range(NJ)]
+        permute_scales(0)
+        for j in range(NJ):
+            x_quant(0, j, x_turn(0, j, pend[j]))
+        permute_scales(1)
+        for j in range(NJ):
+            target(0, j)
+        permute_scales(2)
+        permute_scales(3)
+        for j in range(NJ):
+            target(1, j)
+
+        steps = [(c, f) for c in range(NCH) for f in range(GF)]
+        queue = []
+        avail = {0: 0, 1: 1, 3: 2}
+        for s in range(len(steps) + 1):
+            if s < GF - 1:
+                permute_words(s + 1)
+            if s in (0, 1):
+                for j in (2 * s, 2 * s + 1):
+                    x_quant(1, j, x_turn(1, j, x_scale_rows(1, j)))
+            if 1 <= s:
+                h_quant(*steps[s - 1])
+            if s < len(steps):
+                for t in range(4):
+                    enc(steps[s][0], steps[s][1], t)
+                h_turn(*steps[s])
+            if 1 <= s:
+                c, f = steps[s - 1]
+                if f in avail:
+                    for j in range(NJ):
+                        for dd in range(2):
+                            dec(c, avail[f], j, dd)

@@ -23,7 +23,20 @@ NCH = N // CH
 NJ = CH // P
 GE = D // 512
 GF = F // 512
-OFFLOAD = {(1, 2, 1, 0), (1, 2, 2, 0)}
+OFFLOAD = {(1, 1, 0, 0), (1, 2, 1, 0), (1, 1, 1, 0), (0, 1, 0, 0), (0, 2, 3, 1), (0, 2, 2, 0), (0, 1, 2, 0), (0, 2, 0, 0)}
+WORD = "VVVVVVSS"
+QB = 1
+GRAN = True
+BEATS = [
+    ("m2 Y1 Y7", 2), ("m1", 2), ("m0 Y0 Y2 Y3 Y4 Y6", 0), ("p1 m3 t0 t1 t2 t3", 2),
+    ("p3", 0), ("", 0), ("", 0), ("p2 x1 x2 x3", 2),
+    ("", 2), ("Y5", 1), ("", 1), ("", 1),
+    ("", 1), ("x0", 1), ("", 3), ("", 1),
+    ("", 0), ("", 2), ("", 1), ("", 1),
+    ("", 2), ("", 2), ("", 3), ("", 2),
+    ("", 1), ("", 1), ("", 1), ("", 3),
+    ("", 3), ("", 1), ("", 1), ("", 0),
+]
 
 
 def tile_matryoshkatranscoderresiduals_w4_kernel(
@@ -40,8 +53,12 @@ def tile_matryoshkatranscoderresiduals_w4_kernel(
 
         warm = keep.tile([P, 1], F32)
         ident = keep.tile([P, P], F32)
+        ident_b = keep.tile([P, P], BF16)
+        minus = keep.tile([P, P], BF16)
+        xs8 = keep.tile([P, D // P], F32)
         xscale = keep.tile([P, D], F32)
         benc = keep.tile([P, GF, 4], BF16)
+        brow = keep.tile([P, D], BF16)
         bdec = keep.tile([P, D], BF16)
         xb = [keep.tile([P, NJ, D], U8, name="xb%d" % c) for c in range(NCH)]
         yt = [keep.tile([P, NJ, D], BF16, name="yt%d" % c) for c in range(NCH)]
@@ -54,12 +71,18 @@ def tile_matryoshkatranscoderresiduals_w4_kernel(
         xcod = [keep.tile([P, GE, CH], U32, name="xcod%d" % c, align_bytes=64) for c in range(NCH)]
         xcs = [keep.tile([P, GE, CH], U8, name="xcs%d" % c, align_bytes=64) for c in range(NCH)]
 
+        ctx.enter_context(tc.manual_schedule())
         nc.vector.memset(wsraw[:].rearrange("p g n -> p (g n)").bitcast(I32), 0)
-        nc.vector.memset(wds[:].rearrange("p g n -> p (g n)").bitcast(I32), 0)
         nc.vector.memset(warm[:], 0.0)
-        nc.scalar.dma_start(out=xscale[:], in_=x_scale.rearrange("o k -> (o k)").partition_broadcast(P))
-        nc.scalar.activation(out=warm[:], in_=warm[:], func=ACT.Relu)
         make_identity(nc, ident[:])
+        nc.scalar.dma_start(out=xs8[:], in_=x_scale.rearrange("o (c p) -> p (o c)", p=P))
+        nc.scalar.dma_start(out=benc[:], in_=b_enc.rearrange("(g p t) -> p g t", p=P, t=4))
+        nc.scalar.activation(out=warm[:], in_=warm[:], func=ACT.Relu)
+        nc.gpsimd.memset(brow[:].bitcast(I32), 0)
+        nc.gpsimd.memset(minus[:], -1.0)
+        nc.gpsimd.memset(wds[:].rearrange("p g n -> p (g n)").bitcast(I32), 0)
+        nc.vector.tensor_copy(out=ident_b[:], in_=ident[:])
+        nc.scalar.dma_start(out=brow[0:1, :], in_=b_dec.rearrange("(o k) -> o k", o=1))
 
         xv = [x_bytes[c * CH : (c + 1) * CH, :].rearrange("(p j) k -> p j k", j=NJ) for c in range(NCH)]
         yv = [y[c * CH : (c + 1) * CH, :].rearrange("(p j) k -> p j k", j=NJ) for c in range(NCH)]
@@ -78,15 +101,13 @@ def tile_matryoshkatranscoderresiduals_w4_kernel(
                     in_=src.bitcast(I32)[:, 4 * q : 4 * q + 4, :].rearrange("g q n -> q g n"),
                 )
 
-        nc.scalar.dma_start(out=benc[:], in_=b_enc.rearrange("(g p t) -> p g t", p=P, t=4))
-        nc.scalar.dma_start(out=bdec[:], in_=b_dec.partition_broadcast(P))
         load_w(0)
+        load_scales(wsraw, w_enc_scales)
         nc.sync.dma_start(out=xb[0][:, 0:2, :], in_=xv[0][:, 0:2, :])
         nc.sync.dma_start(out=xb[0][:, 2:4, :], in_=xv[0][:, 2:4, :])
-        load_scales(wsraw, w_enc_scales)
+        nc.sync.dma_start(out=yt[0][:], in_=yv[0])
         load_w(1)
         nc.sync.dma_start(out=xb[1][:], in_=xv[1])
-        nc.sync.dma_start(out=yt[0][:], in_=yv[0])
         load_w(2)
         load_w(3)
         nc.sync.dma_start(out=wd[:, 0:2, :].bitcast(I32), in_=w_dec_words[0:2].bitcast(I32).rearrange("g p n -> p g n"))
@@ -100,141 +121,232 @@ def tile_matryoshkatranscoderresiduals_w4_kernel(
                     out=wperm[f][:, g, :].bitcast(U16).rearrange("p (t m) -> p t m", t=4),
                     in_=wraw[f][:, g, :].bitcast(U16).rearrange("p (m t) -> p t m", t=4),
                 )
+
         def permute_scales(f):
-            (nc.vector if f < 1 else nc.gpsimd).tensor_copy(
+            nc.vector.tensor_copy(
                 out=wsperm[f][:].rearrange("p g (t m) -> p g t m", t=4),
                 in_=wsraw[:, :, f * 512 : (f + 1) * 512].rearrange("p g (m t) -> p g t m", t=4),
             )
 
-        def x_scale_rows(c, j):
-            xs = work.tile([P, D], BF16, name="xs")
-            nc.vector.tensor_tensor(out=xs[:], in0=xb[c][:, j, :].bitcast(FP8), in1=xscale[:], op=ALU.mult)
-            return xs
+        def spread_x_scale():
+            for h in range(2):
+                bank = pd_pool.tile([P, 512], F32, name="pd")
+                for i in range(4):
+                    col = 4 * h + i
+                    nc.tensor.transpose(
+                        bank[:, P * i : P * (i + 1)], xs8[:, col : col + 1].to_broadcast([P, P]), ident[:]
+                    )
+                nc.scalar.copy(out=xscale[:, 512 * h : 512 * (h + 1)], in_=bank[:])
 
-        def x_turn(c, j, xs):
-            bank = pe_pool.tile([P, 4, P], F32, name="pe")
-            words = xs[:].bitcast(F32)
+        xs, xin = {}, {}
+
+        def x_mult(c, j):
+            xs[c, j] = work.tile([P, D], BF16, name="xs", bufs=4)
+            nc.vector.tensor_tensor(out=xs[c, j][:], in0=xb[c][:, j, :].bitcast(FP8), in1=xscale[:], op=ALU.mult)
+
+        def x_turn(c, j):
+            bank = pd_pool.tile([P, 4, P], F32, name="pd")
+            words = xs[c, j][:].bitcast(F32)
             for g in range(GE):
                 for u in range(2):
                     nc.tensor.transpose(bank[:, 2 * g + u, :], words[:, 256 * g + u : 256 * (g + 1) : 2], ident[:])
-            xin = work.tile([P, GE, P, 4], BF16, name="xin", align_bytes=64)
+            xin[c, j] = work.tile([P, GE, P, 4], BF16, name="xin", align_bytes=64, bufs=4)
             nc.scalar.copy(
-                out=xin[:].rearrange("p g n t -> p (g n t)").bitcast(F32).rearrange("p (g n u) -> p g n u", g=GE, u=2),
+                out=xin[c, j][:].rearrange("p g n t -> p (g n t)").bitcast(F32).rearrange("p (g n u) -> p g n u", g=GE, u=2),
                 in_=bank[:].rearrange("p (g u) n -> p g n u", u=2),
             )
-            return xin
 
-        def x_quant(c, j, xin):
+        def x_quant(c, j):
             for g in range(GE):
                 cols = slice(j * P, (j + 1) * P)
                 nc.vector.quantize_mx(
                     out=xcod[c][:, g, cols].bitcast(FP8X4),
                     scales=xcs[c][:, g, cols],
-                    in_=xin[:, g, :, :].rearrange("p n t -> p (n t)"),
+                    in_=xin[c, j][:, g, :, :].rearrange("p n t -> p (n t)"),
                 )
 
-        hcod, hsc = {}, {}
-        hbuf = {}
+        hcod, hsc, hbuf, hin, ebank = {}, {}, {}, {}, {}
 
-        def enc(c, f, t):
-            bank = pe_pool.tile([P, CH], F32, name="pe")
+        def enc(c, f, t, n0=0, n1=CH):
+            if n0 == 0:
+                ebank[c, f, t] = pe_pool.tile([P, CH], F32, name="pe")
             for g in range(GE):
                 nc.tensor.matmul_mx(
-                    out=bank[:],
+                    out=ebank[c, f, t][:, n0:n1],
                     lhsT=wperm[f][:, g, 256 * t : 256 * (t + 1)].bitcast(FP4X4),
                     lhsT_scale=wsperm[f][:, g, 128 * t : 128 * (t + 1)],
-                    rhs=xcod[c][:, g, :].bitcast(FP8X4),
-                    rhs_scale=xcs[c][:, g, :],
+                    rhs=xcod[c][:, g, n0:n1].bitcast(FP8X4),
+                    rhs_scale=xcs[c][:, g, n0:n1],
                     start=(g == 0),
                     stop=(g == GE - 1),
                 )
-            if t == 0:
+
+        def act(c, f, t, n0=0, n1=CH):
+            if t == 0 and n0 == 0:
                 hbuf[c, f] = work.tile([P, 2, CH, 2], BF16, name="hb")
             nc.scalar.activation(
-                out=hbuf[c, f][:, t // 2, :, t % 2], in_=bank[:], func=ACT.Relu, bias=benc[:, f, t : t + 1]
+                out=hbuf[c, f][:, t // 2, n0:n1, t % 2],
+                in_=ebank[c, f, t][:, n0:n1],
+                func=ACT.Relu,
+                bias=benc[:, f, t : t + 1],
             )
 
-        hins = {}
+        def h_turn(c, f, eng, n0=0, n1=CH):
+            if n0 == 0:
+                hin[c, f] = work.tile([P, CH, 4], BF16, name="hin", align_bytes=64)
+            dst = hin[c, f][:].rearrange("p n t -> p (n t)").bitcast(F32).rearrange("p (n u) -> p n u", u=2)[:, n0:n1, :]
+            src = hbuf[c, f][:].rearrange("p u n e -> p (u n e)").bitcast(F32).rearrange("p (u n) -> p n u", u=2)[:, n0:n1, :]
+            if eng == "V":
+                nc.vector.tensor_copy(out=dst, in_=src)
+            else:
+                nc.scalar.copy(out=dst, in_=src)
 
-        def h_turn(c, f):
-            hin = work.tile([P, CH, 4], BF16, name="hin", align_bytes=64)
-            nc.scalar.copy(
-                out=hin[:].rearrange("p n t -> p (n t)").bitcast(F32).rearrange("p (n u) -> p n u", u=2),
-                in_=hbuf[c, f][:].rearrange("p u n e -> p (u n e)").bitcast(F32).rearrange("p (u n) -> p n u", u=2),
-            )
-            hins[c, f] = hin
-
-        def h_quant(c, f):
-            hcod[c, f] = hpool.tile([P, CH], U32, name="hcod", align_bytes=64)
-            hsc[c, f] = hpool.tile([P, CH], U8, name="hsc", align_bytes=64)
+        def h_quant(c, f, n0=0, n1=CH):
+            if n0 == 0:
+                hcod[c, f] = hpool.tile([P, CH], U32, name="hcod", align_bytes=64)
+                hsc[c, f] = hpool.tile([P, CH], U8, name="hsc", align_bytes=64)
             nc.vector.quantize_mx(
-                out=hcod[c, f][:].bitcast(FP8X4), scales=hsc[c, f][:], in_=hins[c, f][:].rearrange("p n t -> p (n t)")
+                out=hcod[c, f][:, n0:n1].bitcast(FP8X4),
+                scales=hsc[c, f][:, n0:n1],
+                in_=hin[c, f][:, n0:n1, :].rearrange("p n t -> p (n t)"),
             )
 
         res = {}
 
-        def target(c, j):
-            t = rpool.tile([P, D], F32, name="tgt")
-            nc.gpsimd.tensor_tensor(out=t[:], in0=yt[c][:, j, :], in1=bdec[:], op=ALU.subtract)
-            res[c, j] = t
+        def spread_b_dec():
+            for dd in range(2):
+                cols = slice(512 * dd, 512 * (dd + 1))
+                bank = pd_pool.tile([P, 512], F32, name="pd")
+                nc.tensor.matmul(bank[:], minus[:], brow[:, cols], start=True, stop=True)
+                nc.scalar.copy(out=bdec[:, cols], in_=bank[:])
 
-        def dec(c, k, j, d):
-            groups = ([0], [1], [2, 3])[k]
+        def target_pe(c, j, dd):
+            cols = slice(512 * dd, 512 * (dd + 1))
+            if (c, j, -1) not in res:
+                res[c, j, -1] = rpool.tile([P, D], F32, name="tgt%d" % c, bufs=4)
             bank = pd_pool.tile([P, 512], F32, name="pd")
-            for i, f in enumerate(groups):
-                nc.tensor.matmul_mx(
-                    out=bank[:],
-                    lhsT=hcod[c, f][:, j * P : (j + 1) * P].bitcast(FP8X4),
-                    lhsT_scale=hsc[c, f][:, j * P : (j + 1) * P],
-                    rhs=wd[:, f, 1024 * d : 1024 * (d + 1)].bitcast(FP4X4),
-                    rhs_scale=wds[:, f, 512 * d : 512 * (d + 1)],
-                    start=(i == 0),
-                    stop=(i == len(groups) - 1),
-                )
+            nc.tensor.matmul(bank[:], ident_b[:], yt[c][:, j, cols], start=True, stop=False)
+            nc.tensor.matmul(bank[:], minus[:], brow[:, cols], start=False, stop=True)
+            nc.scalar.copy(out=res[c, j, -1][:, cols], in_=bank[:])
+
+        def target_pool(c, j, dd):
+            cols = slice(512 * dd, 512 * (dd + 1))
+            if dd == 0:
+                res[c, j, -1] = rpool.tile([P, D], F32, name="tgt%d" % c, bufs=4)
+            nc.gpsimd.tensor_tensor(out=res[c, j, -1][:, cols], in0=yt[c][:, j, cols], in1=bdec[:, cols], op=ALU.add)
+
+        dbank = {}
+        FEATURES = ([0], [1], [2, 3])
+
+        def dec_mm(u, part=None):
+            c, k, j, d = u
+            if part in (None, 0):
+                dbank[u] = pd_pool.tile([P, 512], F32, name="pd")
+            last = len(FEATURES[k]) - 1
+            for i, f in enumerate(FEATURES[k]):
+                if part is None or part == i:
+                    nc.tensor.matmul_mx(
+                        out=dbank[u][:],
+                        lhsT=hcod[c, f][:, j * P : (j + 1) * P].bitcast(FP8X4),
+                        lhsT_scale=hsc[c, f][:, j * P : (j + 1) * P],
+                        rhs=wd[:, f, 1024 * d : 1024 * (d + 1)].bitcast(FP4X4),
+                        rhs_scale=wds[:, f, 512 * d : 512 * (d + 1)],
+                        start=(i == 0),
+                        stop=(i == last),
+                    )
+
+        def dec_out(u):
+            c, k, j, d = u
             if d == 0:
                 res[c, j, k] = rpool.tile([P, D], F32, name="r%d" % k)
-            prev = res[c, j] if k == 0 else res[c, j, k - 1]
             cols = slice(512 * d, 512 * (d + 1))
-            if (c, k, j, d) in OFFLOAD:
-                part = work.tile([P, 512], F32, name="part")
-                nc.scalar.copy(out=part[:], in_=bank[:])
-                nc.gpsimd.tensor_tensor(out=res[c, j, k][:, cols], in0=prev[:, cols], in1=part[:], op=ALU.subtract)
+            prev = res[c, j, k - 1][:, cols]
+            if u in OFFLOAD:
+                part = work.tile([P, 512], F32, name="part", bufs=2)
+                nc.scalar.copy(out=part[:], in_=dbank[u][:])
+                nc.gpsimd.tensor_tensor(out=res[c, j, k][:, cols], in0=prev, in1=part[:], op=ALU.subtract)
             else:
-                nc.vector.tensor_tensor(out=res[c, j, k][:, cols], in0=prev[:, cols], in1=bank[:], op=ALU.subtract)
+                nc.vector.tensor_tensor(out=res[c, j, k][:, cols], in0=prev, in1=dbank[u][:], op=ALU.subtract)
             if d == 1:
                 nc.sync.dma_start(out=ov[k][c][:, j, :], in_=res[c, j, k][:])
 
+        def permute(f):
+            permute_scales(f)
+            permute_words(f)
+
+        side = {
+            "m": lambda i: x_mult(1, i),
+            "t": lambda i: x_turn(1, i),
+            "x": lambda i: x_quant(1, i),
+            "p": permute,
+            "Y": lambda i: target_pe(0, i // 2, i % 2),
+        }
+
+        spread_x_scale()
         permute_words(0)
-        pend = [x_scale_rows(0, j) for j in range(NJ)]
         permute_scales(0)
         for j in range(NJ):
-            x_quant(0, j, x_turn(0, j, pend[j]))
-        permute_scales(1)
+            x_mult(0, j)
+            x_turn(0, j)
+            if j >= 1:
+                x_quant(0, j - 1)
+            if GRAN and j >= 2:
+                for t in range(4):
+                    enc(0, 0, t, P * (j - 2), P * (j - 1))
+        if GRAN:
+            for t in range(4):
+                act(0, 0, t, 0, 256)
+            for t in range(4):
+                enc(0, 0, t, 256, 384)
+        x_quant(0, 3)
+        if GRAN:
+            for t in range(4):
+                enc(0, 0, t, 384, 512)
+            for t in range(4):
+                act(0, 0, t, 256, 512)
+        spread_b_dec()
         for j in range(NJ):
-            target(0, j)
-        permute_scales(2)
-        permute_scales(3)
-        for j in range(NJ):
-            target(1, j)
+            for dd in range(2):
+                target_pool(1, j, dd)
 
         steps = [(c, f) for c in range(NCH) for f in range(GF)]
         queue = []
-        avail = {0: 0, 1: 1, 3: 2}
-        for s in range(len(steps) + 1):
-            if s < GF - 1:
-                permute_words(s + 1)
-            if s in (0, 1):
-                for j in (2 * s, 2 * s + 1):
-                    x_quant(1, j, x_turn(1, j, x_scale_rows(1, j)))
-            if 1 <= s:
-                h_quant(*steps[s - 1])
-            if s < len(steps):
-                for t in range(4):
-                    enc(steps[s][0], steps[s][1], t)
-                h_turn(*steps[s])
-            if 1 <= s:
-                c, f = steps[s - 1]
-                if f in avail:
-                    for j in range(NJ):
-                        for dd in range(2):
-                            dec(c, avail[f], j, dd)
+        block = {0: 0, 1: 1, 3: 2}
+        for s, (c, f) in enumerate(steps):
+            for t in range(4):
+                jobs, units = BEATS[4 * s + t]
+                if s > 0 or not GRAN:
+                    enc(c, f, t)
+                if s > 0 and t == QB:
+                    cq, fq = steps[s - 1]
+                    h_quant(cq, fq)
+                    if fq in block:
+                        queue += [(cq, block[fq], j, dd) for j in range(NJ) for dd in range(2)]
+                if 0 < s < 7 or (s == 0 and not GRAN):
+                    act(c, f, t)
+                for job in jobs.split():
+                    side[job[0]](int(job[1:]))
+                for u in queue[:units]:
+                    dec_mm(u)
+                    dec_out(u)
+                queue = queue[units:]
+            if s < 7:
+                h_turn(c, f, WORD[s])
+        for n0 in (0, 256):
+            for t in range(4):
+                act(1, 3, t, n0, n0 + 256)
+            h_turn(1, 3, WORD[7], n0, n0 + 256)
+        for u in queue:
+            dec_mm(u)
+            dec_out(u)
+        last = [(1, 2, j, dd) for j in range(NJ) for dd in range(2)]
+        for u in last[:4]:
+            dec_mm(u, 0)
+        h_quant(1, 3, 0, 256)
+        for u in last[:4]:
+            dec_mm(u, 1)
+            dec_out(u)
+        h_quant(1, 3, 256, 512)
+        for u in last[4:]:
+            dec_mm(u)
+            dec_out(u)

from contextlib import ExitStack

import concourse.mybir as mybir
from concourse.masks import make_identity

F32 = mybir.dt.float32
BF16 = mybir.dt.bfloat16
U8 = mybir.dt.uint8
U16 = mybir.dt.uint16
U32 = mybir.dt.uint32
I32 = mybir.dt.int32
FP8 = mybir.dt.float8_e4m3fn
FP8X4 = mybir.dt.float8_e4m3fn_x4
FP4X4 = mybir.dt.float4_e2m1fn_x4
ALU = mybir.AluOpType
ACT = mybir.ActivationFunctionType

N, D, F = 1024, 1024, 2048
FLOPS = 2 * N * D * F * 2
P = 128
CH = 512
NCH = N // CH
NJ = CH // P
GE = D // 512
GF = F // 512
OFFLOAD = {(1, 1, 0, 0), (1, 2, 1, 0), (1, 1, 1, 0), (0, 1, 0, 0), (0, 2, 3, 1), (0, 2, 2, 0), (0, 1, 2, 0), (0, 2, 0, 0)}
WORD = "VVVVVVSS"
QB = 1
GRAN = True
BEATS = [
    ("m2 Y1 Y7", 2), ("m1", 2), ("m0 Y0 Y2 Y3 Y4 Y6", 0), ("p1 m3 t0 t1 t2 t3", 2),
    ("p3", 0), ("", 0), ("", 0), ("p2 x1 x2 x3", 2),
    ("", 2), ("Y5", 1), ("", 1), ("", 1),
    ("", 1), ("x0", 1), ("", 3), ("", 1),
    ("", 0), ("", 2), ("", 1), ("", 1),
    ("", 2), ("", 2), ("", 3), ("", 2),
    ("", 1), ("", 1), ("", 1), ("", 3),
    ("", 3), ("", 1), ("", 1), ("", 0),
]


def tile_matryoshkatranscoderresiduals_w4_kernel(
    tc, x_bytes, x_scale, w_enc_words, w_enc_scales, b_enc, w_dec_words, w_dec_scales, b_dec, y, out
):
    nc = tc.nc
    with ExitStack() as ctx:
        keep = ctx.enter_context(tc.tile_pool(name="keep", bufs=1))
        work = ctx.enter_context(tc.tile_pool(name="work", bufs=3))
        hpool = ctx.enter_context(tc.tile_pool(name="hpool", bufs=5))
        rpool = ctx.enter_context(tc.tile_pool(name="rpool", bufs=5))
        pe_pool = ctx.enter_context(tc.psum_pool(name="pe_pool", bufs=4))
        pd_pool = ctx.enter_context(tc.psum_pool(name="pd_pool", bufs=4))

        warm = keep.tile([P, 1], F32)
        ident = keep.tile([P, P], F32)
        ident_b = keep.tile([P, P], BF16)
        minus = keep.tile([P, P], BF16)
        xs8 = keep.tile([P, D // P], F32)
        xscale = keep.tile([P, D], F32)
        benc = keep.tile([P, GF, 4], BF16)
        brow = keep.tile([P, D], BF16)
        bdec = keep.tile([P, D], BF16)
        xb = [keep.tile([P, NJ, D], U8, name="xb%d" % c) for c in range(NCH)]
        yt = [keep.tile([P, NJ, D], BF16, name="yt%d" % c) for c in range(NCH)]
        wraw = [keep.tile([P, GE, 1024], U8, name="wraw%d" % f) for f in range(GF)]
        wperm = [keep.tile([P, GE, 1024], U8, name="wperm%d" % f, align_bytes=64) for f in range(GF)]
        wsraw = keep.tile([P, GE, F], U8)
        wsperm = [keep.tile([P, GE, 512], U8, name="wsperm%d" % f, align_bytes=64) for f in range(GF)]
        wd = keep.tile([P, GF, 2 * D], U8, align_bytes=64)
        wds = keep.tile([P, GF, D], U8, align_bytes=64)
        xcod = [keep.tile([P, GE, CH], U32, name="xcod%d" % c, align_bytes=64) for c in range(NCH)]
        xcs = [keep.tile([P, GE, CH], U8, name="xcs%d" % c, align_bytes=64) for c in range(NCH)]

        ctx.enter_context(tc.manual_schedule())
        nc.vector.memset(wsraw[:].rearrange("p g n -> p (g n)").bitcast(I32), 0)
        nc.vector.memset(warm[:], 0.0)
        make_identity(nc, ident[:])
        nc.scalar.dma_start(out=xs8[:], in_=x_scale.rearrange("o (c p) -> p (o c)", p=P))
        nc.scalar.dma_start(out=benc[:], in_=b_enc.rearrange("(g p t) -> p g t", p=P, t=4))
        nc.scalar.activation(out=warm[:], in_=warm[:], func=ACT.Relu)
        nc.gpsimd.memset(brow[:].bitcast(I32), 0)
        nc.gpsimd.memset(minus[:], -1.0)
        nc.gpsimd.memset(wds[:].rearrange("p g n -> p (g n)").bitcast(I32), 0)
        nc.vector.tensor_copy(out=ident_b[:], in_=ident[:])
        nc.scalar.dma_start(out=brow[0:1, :], in_=b_dec.rearrange("(o k) -> o k", o=1))

        xv = [x_bytes[c * CH : (c + 1) * CH, :].rearrange("(p j) k -> p j k", j=NJ) for c in range(NCH)]
        yv = [y[c * CH : (c + 1) * CH, :].rearrange("(p j) k -> p j k", j=NJ) for c in range(NCH)]
        ov = [[out[k, c * CH : (c + 1) * CH, :].rearrange("(p j) k -> p j k", j=NJ) for c in range(NCH)] for k in range(3)]

        def load_w(f):
            nc.sync.dma_start(
                out=wraw[f][:].bitcast(I32),
                in_=w_enc_words.bitcast(I32)[:, :, f * 256 : (f + 1) * 256].rearrange("g p n -> p g n"),
            )

        def load_scales(tile, src):
            for q in range(4):
                nc.sync.dma_start(
                    out=tile[32 * q : 32 * q + 4].bitcast(I32),
                    in_=src.bitcast(I32)[:, 4 * q : 4 * q + 4, :].rearrange("g q n -> q g n"),
                )

        load_w(0)
        load_scales(wsraw, w_enc_scales)
        nc.sync.dma_start(out=xb[0][:, 0:2, :], in_=xv[0][:, 0:2, :])
        nc.sync.dma_start(out=xb[0][:, 2:4, :], in_=xv[0][:, 2:4, :])
        nc.sync.dma_start(out=yt[0][:], in_=yv[0])
        load_w(1)
        nc.sync.dma_start(out=xb[1][:], in_=xv[1])
        load_w(2)
        load_w(3)
        nc.sync.dma_start(out=wd[:, 0:2, :].bitcast(I32), in_=w_dec_words[0:2].bitcast(I32).rearrange("g p n -> p g n"))
        load_scales(wds, w_dec_scales)
        nc.sync.dma_start(out=wd[:, 2:4, :].bitcast(I32), in_=w_dec_words[2:4].bitcast(I32).rearrange("g p n -> p g n"))
        nc.sync.dma_start(out=yt[1][:], in_=yv[1])

        def permute_words(f):
            for g in range(GE):
                nc.vector.tensor_copy(
                    out=wperm[f][:, g, :].bitcast(U16).rearrange("p (t m) -> p t m", t=4),
                    in_=wraw[f][:, g, :].bitcast(U16).rearrange("p (m t) -> p t m", t=4),
                )

        def permute_scales(f):
            nc.vector.tensor_copy(
                out=wsperm[f][:].rearrange("p g (t m) -> p g t m", t=4),
                in_=wsraw[:, :, f * 512 : (f + 1) * 512].rearrange("p g (m t) -> p g t m", t=4),
            )

        def spread_x_scale():
            for h in range(2):
                bank = pd_pool.tile([P, 512], F32, name="pd")
                for i in range(4):
                    col = 4 * h + i
                    nc.tensor.transpose(
                        bank[:, P * i : P * (i + 1)], xs8[:, col : col + 1].to_broadcast([P, P]), ident[:]
                    )
                nc.scalar.copy(out=xscale[:, 512 * h : 512 * (h + 1)], in_=bank[:])

        xs, xin = {}, {}

        def x_mult(c, j):
            xs[c, j] = work.tile([P, D], BF16, name="xs", bufs=4)
            nc.vector.tensor_tensor(out=xs[c, j][:], in0=xb[c][:, j, :].bitcast(FP8), in1=xscale[:], op=ALU.mult)

        def x_turn(c, j):
            bank = pd_pool.tile([P, 4, P], F32, name="pd")
            words = xs[c, j][:].bitcast(F32)
            for g in range(GE):
                for u in range(2):
                    nc.tensor.transpose(bank[:, 2 * g + u, :], words[:, 256 * g + u : 256 * (g + 1) : 2], ident[:])
            xin[c, j] = work.tile([P, GE, P, 4], BF16, name="xin", align_bytes=64, bufs=4)
            nc.scalar.copy(
                out=xin[c, j][:].rearrange("p g n t -> p (g n t)").bitcast(F32).rearrange("p (g n u) -> p g n u", g=GE, u=2),
                in_=bank[:].rearrange("p (g u) n -> p g n u", u=2),
            )

        def x_quant(c, j):
            for g in range(GE):
                cols = slice(j * P, (j + 1) * P)
                nc.vector.quantize_mx(
                    out=xcod[c][:, g, cols].bitcast(FP8X4),
                    scales=xcs[c][:, g, cols],
                    in_=xin[c, j][:, g, :, :].rearrange("p n t -> p (n t)"),
                )

        hcod, hsc, hbuf, hin, ebank = {}, {}, {}, {}, {}

        def enc(c, f, t, n0=0, n1=CH):
            if n0 == 0:
                ebank[c, f, t] = pe_pool.tile([P, CH], F32, name="pe")
            for g in range(GE):
                nc.tensor.matmul_mx(
                    out=ebank[c, f, t][:, n0:n1],
                    lhsT=wperm[f][:, g, 256 * t : 256 * (t + 1)].bitcast(FP4X4),
                    lhsT_scale=wsperm[f][:, g, 128 * t : 128 * (t + 1)],
                    rhs=xcod[c][:, g, n0:n1].bitcast(FP8X4),
                    rhs_scale=xcs[c][:, g, n0:n1],
                    start=(g == 0),
                    stop=(g == GE - 1),
                )

        def act(c, f, t, n0=0, n1=CH):
            if t == 0 and n0 == 0:
                hbuf[c, f] = work.tile([P, 2, CH, 2], BF16, name="hb")
            nc.scalar.activation(
                out=hbuf[c, f][:, t // 2, n0:n1, t % 2],
                in_=ebank[c, f, t][:, n0:n1],
                func=ACT.Relu,
                bias=benc[:, f, t : t + 1],
            )

        def h_turn(c, f, eng, n0=0, n1=CH):
            if n0 == 0:
                hin[c, f] = work.tile([P, CH, 4], BF16, name="hin", align_bytes=64)
            dst = hin[c, f][:].rearrange("p n t -> p (n t)").bitcast(F32).rearrange("p (n u) -> p n u", u=2)[:, n0:n1, :]
            src = hbuf[c, f][:].rearrange("p u n e -> p (u n e)").bitcast(F32).rearrange("p (u n) -> p n u", u=2)[:, n0:n1, :]
            if eng == "V":
                nc.vector.tensor_copy(out=dst, in_=src)
            else:
                nc.scalar.copy(out=dst, in_=src)

        def h_quant(c, f, n0=0, n1=CH):
            if n0 == 0:
                hcod[c, f] = hpool.tile([P, CH], U32, name="hcod", align_bytes=64)
                hsc[c, f] = hpool.tile([P, CH], U8, name="hsc", align_bytes=64)
            nc.vector.quantize_mx(
                out=hcod[c, f][:, n0:n1].bitcast(FP8X4),
                scales=hsc[c, f][:, n0:n1],
                in_=hin[c, f][:, n0:n1, :].rearrange("p n t -> p (n t)"),
            )

        res = {}

        def spread_b_dec():
            for dd in range(2):
                cols = slice(512 * dd, 512 * (dd + 1))
                bank = pd_pool.tile([P, 512], F32, name="pd")
                nc.tensor.matmul(bank[:], minus[:], brow[:, cols], start=True, stop=True)
                nc.scalar.copy(out=bdec[:, cols], in_=bank[:])

        def target_pe(c, j, dd):
            cols = slice(512 * dd, 512 * (dd + 1))
            if (c, j, -1) not in res:
                res[c, j, -1] = rpool.tile([P, D], F32, name="tgt%d" % c, bufs=4)
            bank = pd_pool.tile([P, 512], F32, name="pd")
            nc.tensor.matmul(bank[:], ident_b[:], yt[c][:, j, cols], start=True, stop=False)
            nc.tensor.matmul(bank[:], minus[:], brow[:, cols], start=False, stop=True)
            nc.scalar.copy(out=res[c, j, -1][:, cols], in_=bank[:])

        def target_pool(c, j, dd):
            cols = slice(512 * dd, 512 * (dd + 1))
            if dd == 0:
                res[c, j, -1] = rpool.tile([P, D], F32, name="tgt%d" % c, bufs=4)
            nc.gpsimd.tensor_tensor(out=res[c, j, -1][:, cols], in0=yt[c][:, j, cols], in1=bdec[:, cols], op=ALU.add)

        dbank = {}
        FEATURES = ([0], [1], [2, 3])

        def dec_mm(u, part=None):
            c, k, j, d = u
            if part in (None, 0):
                dbank[u] = pd_pool.tile([P, 512], F32, name="pd")
            last = len(FEATURES[k]) - 1
            for i, f in enumerate(FEATURES[k]):
                if part is None or part == i:
                    nc.tensor.matmul_mx(
                        out=dbank[u][:],
                        lhsT=hcod[c, f][:, j * P : (j + 1) * P].bitcast(FP8X4),
                        lhsT_scale=hsc[c, f][:, j * P : (j + 1) * P],
                        rhs=wd[:, f, 1024 * d : 1024 * (d + 1)].bitcast(FP4X4),
                        rhs_scale=wds[:, f, 512 * d : 512 * (d + 1)],
                        start=(i == 0),
                        stop=(i == last),
                    )

        def dec_out(u):
            c, k, j, d = u
            if d == 0:
                res[c, j, k] = rpool.tile([P, D], F32, name="r%d" % k)
            cols = slice(512 * d, 512 * (d + 1))
            prev = res[c, j, k - 1][:, cols]
            if u in OFFLOAD:
                part = work.tile([P, 512], F32, name="part", bufs=2)
                nc.scalar.copy(out=part[:], in_=dbank[u][:])
                nc.gpsimd.tensor_tensor(out=res[c, j, k][:, cols], in0=prev, in1=part[:], op=ALU.subtract)
            else:
                nc.vector.tensor_tensor(out=res[c, j, k][:, cols], in0=prev, in1=dbank[u][:], op=ALU.subtract)
            if d == 1:
                nc.sync.dma_start(out=ov[k][c][:, j, :], in_=res[c, j, k][:])

        def permute(f):
            permute_scales(f)
            permute_words(f)

        side = {
            "m": lambda i: x_mult(1, i),
            "t": lambda i: x_turn(1, i),
            "x": lambda i: x_quant(1, i),
            "p": permute,
            "Y": lambda i: target_pe(0, i // 2, i % 2),
        }

        spread_x_scale()
        permute_words(0)
        permute_scales(0)
        for j in range(NJ):
            x_mult(0, j)
            x_turn(0, j)
            if j >= 1:
                x_quant(0, j - 1)
            if GRAN and j >= 2:
                for t in range(4):
                    enc(0, 0, t, P * (j - 2), P * (j - 1))
        if GRAN:
            for t in range(4):
                act(0, 0, t, 0, 256)
            for t in range(4):
                enc(0, 0, t, 256, 384)
        x_quant(0, 3)
        if GRAN:
            for t in range(4):
                enc(0, 0, t, 384, 512)
            for t in range(4):
                act(0, 0, t, 256, 512)
        spread_b_dec()
        for j in range(NJ):
            for dd in range(2):
                target_pool(1, j, dd)

        steps = [(c, f) for c in range(NCH) for f in range(GF)]
        queue = []
        block = {0: 0, 1: 1, 3: 2}
        for s, (c, f) in enumerate(steps):
            for t in range(4):
                jobs, units = BEATS[4 * s + t]
                if s > 0 or not GRAN:
                    enc(c, f, t)
                if s > 0 and t == QB:
                    cq, fq = steps[s - 1]
                    h_quant(cq, fq)
                    if fq in block:
                        queue += [(cq, block[fq], j, dd) for j in range(NJ) for dd in range(2)]
                if 0 < s < 7 or (s == 0 and not GRAN):
                    act(c, f, t)
                for job in jobs.split():
                    side[job[0]](int(job[1:]))
                for u in queue[:units]:
                    dec_mm(u)
                    dec_out(u)
                queue = queue[units:]
            if s < 7:
                h_turn(c, f, WORD[s])
        for n0 in (0, 256):
            for t in range(4):
                act(1, 3, t, n0, n0 + 256)
            h_turn(1, 3, WORD[7], n0, n0 + 256)
        for u in queue:
            dec_mm(u)
            dec_out(u)
        last = [(1, 2, j, dd) for j in range(NJ) for dd in range(2)]
        for u in last[:4]:
            dec_mm(u, 0)
        h_quant(1, 3, 0, 256)
        for u in last[:4]:
            dec_mm(u, 1)
            dec_out(u)
        h_quant(1, 3, 256, 512)
        for u in last[4:]:
            dec_mm(u)
            dec_out(u)
